import numpy as np, ml_dtypes
CORES = [7,15,23,31,167,175,183,191,327,335,343,351,487,495,503,511]
N = 16
TOK = 64
ROUTE = [[[1,15],[6,14],[12,14],[3,14],[11,14],[1,14],[0,14],[1,14],[6,14],[13,14],[14,15],[11,12],[10,14],[8,14],[5,7],[4,8],[0,12],[11,14],[13,14],[0,6],[0,4],[2,4],[5,14],[0,14],[5,11],[9,14],[11,14],[13,14],[0,14],[10,14],[1,3],[9,14],[4,5],[11,14],[7,14],[11,14],[13,14],[2,7],[1,14],[7,15],[13,14],[10,14],[10,14],[4,14],[6,14],[6,9],[0,6],[2,14],[8,12],[2,11],[9,14],[11,14],[7,14],[1,10],[9,14],[5,14],[6,14],[0,12],[7,12],[2,14],[6,8],[13,14],[10,14],[6,14]],[[2,14],[6,14],[3,14],[10,14],[1,14],[5,14],[0,10],[1,14],[10,14],[3,14],[0,15],[11,14],[5,14],[9,11],[12,14],[6,8],[1,10],[8,15],[13,14],[8,14],[3,14],[2,14],[1,14],[3,14],[5,11],[6,14],[13,14],[1,9],[0,14],[12,14],[0,3],[3,14],[6,14],[4,13],[0,14],[3,14],[13,14],[4,14],[7,9],[2,6],[12,13],[14,15],[12,14],[2,14],[1,14],[7,14],[5,10],[5,14],[9,14],[10,14],[8,14],[0,7],[10,11],[7,14],[12,14],[5,8],[12,14],[10,14],[0,14],[9,14],[11,14],[11,14],[13,14],[2,14]],[[1,14],[5,6],[4,14],[8,12],[13,14],[2,14],[13,14],[4,14],[10,14],[0,1],[0,14],[1,11],[0,14],[3,10],[5,6],[14,15],[4,14],[11,12],[6,14],[13,14],[4,15],[8,10],[9,13],[4,14],[4,14],[9,14],[10,14],[3,9],[1,14],[11,14],[8,10],[3,14],[3,14],[3,14],[1,14],[11,14],[14,15],[3,8],[7,12],[3,5],[5,9],[6,14],[5,7],[5,7],[6,14],[8,10],[9,14],[0,1],[1,2],[7,12],[7,12],[12,14],[4,6],[0,15],[2,11],[14,15],[13,15],[4,14],[1,7],[2,15],[8,14],[14,15],[9,14],[0,14]],[[5,14],[6,8],[11,14],[9,14],[4,14],[0,12],[0,14],[9,14],[7,14],[2,7],[12,14],[5,12],[1,11],[1,6],[0,5],[13,14],[2,14],[10,13],[13,14],[12,14],[0,4],[13,14],[5,14],[2,15],[6,8],[3,9],[7,14],[5,14],[1,14],[3,8],[14,15],[3,14],[2,14],[14,15],[6,9],[4,14],[2,12],[3,14],[2,15],[3,4],[0,8],[9,14],[2,14],[12,14],[5,14],[8,9],[2,14],[5,14],[3,14],[4,14],[7,14],[7,14],[1,14],[2,9],[13,14],[6,14],[6,7],[2,7],[1,14],[11,14],[14,15],[7,8],[7,14],[12,14]],[[11,14],[10,15],[1,14],[2,4],[0,14],[14,15],[5,14],[3,4],[8,14],[7,11],[3,14],[2,14],[1,8],[6,14],[7,8],[13,14],[3,12],[0,14],[1,14],[6,15],[9,14],[7,15],[8,14],[4,8],[4,5],[8,14],[2,7],[8,14],[9,14],[2,11],[9,11],[6,14],[6,14],[1,14],[9,11],[2,10],[4,14],[6,14],[5,9],[5,14],[11,14],[1,6],[11,14],[6,14],[0,14],[2,14],[10,15],[5,14],[8,14],[6,9],[5,14],[12,14],[5,14],[6,14],[4,14],[6,10],[5,9],[7,14],[2,4],[4,14],[10,15],[10,14],[13,14],[1,12]],[[11,14],[1,12],[5,14],[6,14],[10,14],[12,14],[0,11],[1,12],[12,14],[9,14],[2,10],[4,12],[4,7],[4,8],[7,14],[13,14],[3,4],[3,4],[6,14],[0,14],[1,14],[2,14],[10,14],[10,14],[0,15],[0,6],[0,15],[12,14],[8,14],[9,14],[9,14],[5,14],[9,14],[12,14],[9,14],[1,14],[7,14],[9,14],[4,8],[5,14],[7,14],[4,14],[4,7],[6,14],[11,14],[2,14],[6,14],[1,5],[10,14],[1,2],[6,14],[3,15],[6,8],[2,12],[4,12],[6,10],[7,12],[2,4],[13,14],[2,7],[10,14],[4,14],[0,14],[2,14]],[[14,15],[0,1],[14,15],[0,5],[10,14],[1,14],[2,14],[8,14],[4,13],[6,14],[11,14],[6,14],[1,5],[6,14],[1,5],[4,9],[10,14],[9,13],[11,13],[9,14],[0,14],[6,14],[1,6],[9,14],[10,14],[2,14],[9,14],[7,14],[5,6],[10,14],[9,14],[14,15],[3,10],[3,14],[8,14],[1,10],[7,14],[8,15],[9,14],[3,13],[4,14],[9,12],[14,15],[4,14],[9,14],[4,6],[13,14],[14,15],[12,14],[7,9],[7,14],[9,14],[3,5],[2,14],[10,14],[9,14],[1,2],[1,14],[13,14],[7,14],[13,14],[1,6],[8,14],[6,14]],[[14,15],[7,12],[5,14],[3,14],[3,4],[5,14],[4,14],[1,14],[3,4],[0,14],[4,15],[6,15],[2,14],[8,14],[9,12],[3,15],[10,15],[7,14],[8,14],[0,14],[6,14],[0,14],[11,13],[7,10],[9,14],[0,12],[13,14],[5,11],[8,14],[1,14],[5,10],[8,14],[7,14],[3,14],[11,14],[1,5],[12,14],[2,7],[5,10],[1,14],[12,14],[5,14],[14,15],[9,14],[7,11],[2,10],[0,8],[12,14],[2,11],[14,15],[9,14],[2,7],[3,14],[12,14],[2,14],[5,9],[0,14],[1,14],[10,12],[0,1],[10,13],[14,15],[1,3],[7,14]],[[12,14],[8,14],[0,14],[5,14],[13,14],[10,14],[6,13],[11,14],[0,11],[2,15],[2,14],[1,14],[6,8],[3,8],[4,6],[6,10],[2,14],[6,7],[9,12],[6,14],[3,12],[2,10],[6,14],[1,14],[1,14],[11,13],[4,12],[13,14],[3,14],[2,14],[12,14],[12,13],[3,14],[3,14],[14,15],[8,9],[4,12],[7,14],[12,14],[7,14],[9,11],[11,14],[4,14],[9,14],[12,14],[1,14],[7,14],[8,14],[1,14],[2,13],[12,14],[2,14],[0,13],[4,14],[6,14],[9,11],[0,2],[3,15],[2,14],[11,14],[0,14],[1,14],[3,8],[9,11]],[[7,10],[0,14],[0,2],[9,14],[13,14],[10,14],[4,14],[11,14],[1,14],[0,6],[8,13],[13,14],[3,14],[10,14],[5,11],[2,14],[0,14],[10,14],[6,14],[13,14],[2,14],[12,14],[14,15],[12,14],[2,14],[4,6],[5,10],[2,13],[8,9],[14,15],[12,14],[5,14],[8,14],[2,14],[9,13],[13,14],[2,14],[2,10],[0,14],[6,14],[3,11],[3,10],[3,12],[5,6],[0,1],[5,9],[6,10],[11,14],[8,13],[0,15],[1,6],[5,12],[4,6],[6,14],[14,15],[6,14],[4,14],[3,5],[10,14],[8,10],[10,14],[3,14],[7,14],[11,14]],[[1,2],[0,14],[7,14],[8,14],[0,5],[3,14],[11,14],[0,11],[7,14],[7,14],[8,14],[2,14],[10,14],[1,6],[9,13],[1,14],[6,8],[9,13],[3,14],[7,14],[3,14],[3,7],[7,8],[0,8],[2,9],[11,14],[12,14],[2,14],[3,14],[1,14],[9,14],[10,14],[0,10],[8,14],[10,14],[4,14],[4,14],[3,14],[6,14],[4,6],[14,15],[1,7],[11,14],[1,8],[3,14],[4,14],[4,14],[6,14],[14,15],[3,4],[9,14],[11,14],[13,14],[12,14],[14,15],[2,4],[8,14],[14,15],[0,4],[2,14],[1,7],[9,14],[2,14],[9,14]],[[6,14],[0,7],[2,3],[12,14],[0,14],[13,14],[0,14],[10,15],[3,14],[9,14],[3,9],[6,15],[9,14],[4,6],[0,14],[0,11],[4,14],[5,10],[5,11],[7,8],[7,13],[4,7],[4,8],[7,14],[14,15],[4,14],[7,14],[2,4],[3,14],[10,14],[7,14],[2,14],[4,14],[2,15],[9,14],[2,14],[11,14],[1,14],[7,14],[2,6],[8,14],[12,14],[3,14],[1,14],[6,14],[9,14],[6,14],[0,5],[12,14],[13,14],[2,10],[2,14],[0,9],[3,14],[6,14],[3,14],[2,8],[5,14],[12,14],[8,13],[8,14],[1,13],[11,15],[1,8]],[[4,14],[5,10],[14,15],[0,14],[11,14],[9,14],[2,5],[11,14],[13,14],[8,14],[9,14],[0,14],[4,11],[1,14],[6,14],[4,8],[8,14],[0,14],[13,14],[0,15],[5,13],[6,8],[0,2],[7,14],[5,6],[1,11],[1,8],[5,14],[8,14],[0,13],[6,9],[4,10],[6,14],[0,1],[2,6],[13,14],[9,14],[4,14],[3,14],[8,15],[2,11],[2,14],[10,14],[9,14],[1,4],[10,11],[10,12],[2,11],[7,12],[3,14],[8,11],[14,15],[10,11],[3,14],[3,11],[6,14],[2,15],[3,13],[5,12],[2,12],[11,14],[0,15],[9,14],[9,14]],[[6,14],[2,9],[12,14],[2,14],[9,11],[14,15],[12,14],[0,2],[8,14],[4,14],[7,14],[11,14],[1,14],[2,14],[8,14],[4,5],[6,14],[8,14],[1,4],[3,15],[4,14],[11,14],[1,15],[4,14],[8,14],[6,14],[3,11],[5,14],[1,12],[12,14],[0,8],[11,14],[1,14],[8,14],[7,14],[2,6],[3,14],[1,14],[5,14],[3,14],[4,14],[8,14],[10,14],[2,14],[2,14],[6,7],[10,14],[8,12],[0,14],[2,7],[0,1],[6,9],[9,14],[10,11],[13,14],[14,15],[2,6],[8,14],[2,14],[10,14],[2,14],[14,15],[9,14],[7,14]],[[1,14],[6,13],[3,4],[6,14],[1,14],[4,14],[11,14],[6,14],[0,14],[9,14],[3,14],[9,14],[5,14],[14,15],[11,14],[12,13],[5,14],[12,14],[11,14],[4,12],[4,12],[14,15],[8,14],[10,14],[3,10],[12,14],[0,7],[8,14],[11,14],[2,14],[11,12],[2,14],[2,5],[5,14],[10,15],[7,8],[10,14],[2,14],[14,15],[7,12],[4,14],[11,14],[1,6],[2,14],[0,2],[14,15],[6,14],[12,14],[5,14],[4,5],[4,14],[5,14],[2,14],[4,14],[12,14],[4,15],[8,14],[10,14],[0,11],[13,14],[9,14],[14,15],[5,11],[4,9]],[[9,14],[14,15],[7,14],[11,13],[7,14],[9,14],[0,15],[7,10],[1,9],[5,14],[5,15],[7,9],[5,14],[2,14],[6,14],[12,14],[11,14],[7,13],[2,14],[1,4],[12,14],[3,14],[12,14],[1,5],[8,14],[1,7],[2,15],[7,8],[8,14],[6,13],[6,14],[4,13],[8,9],[4,13],[1,14],[2,14],[11,14],[8,10],[6,14],[5,14],[6,14],[13,14],[5,14],[12,14],[1,12],[3,14],[4,15],[2,7],[14,15],[8,10],[4,14],[7,14],[2,14],[9,14],[0,14],[1,5],[2,14],[6,15],[8,10],[4,14],[2,5],[0,10],[10,14],[3,14]]]
def setup_inputs(rng):
    return {"x": rng.standard_normal((N, 128, TOK), dtype=np.float32).astype(ml_dtypes.bfloat16), "w": rng.standard_normal((N, 128, 128), dtype=np.float32).astype(ml_dtypes.bfloat16)}
def reference(x, w):
    X, W = x.astype(np.float64), w.astype(np.float64)
    y = np.zeros((N, 128, TOK))
    for r in range(N):
        for t in range(TOK):
            for e in ROUTE[r][t]:
                y[r][:, t] += W[e].T @ X[r][:, t]
    return {"y": y.astype(ml_dtypes.bfloat16 if x.dtype != np.float64 else np.float64)}

@@ -1,0 +1,188 @@
+from concourse.bass import DstId, RemoteDMATransfer
+from concourse.mybir import AluOpType
+
+NEXP = 16
+D = 128
+NFAR = 2
+SCRATCH = {
+    "wall": ("sbuf", [D, NEXP * D], "bfloat16"),
+    "wd": ("dram", [D, D], "bfloat16"),
+    "xs": ("sbuf", [D, 64], "bfloat16"),
+    "tmp": ("sbuf", [D, 64], "float32"),
+    "ys": ("sbuf", [D, 64], "bfloat16"),
+    "p1": ("psum", [D, 512], "float32"),
+    "p2": ("psum", [D, 512], "float32"),
+}
+SEMAPHORES = ["wa%d" % e for e in range(NEXP)] + ["wdl", "wl", "xl", "sent", "m1", "m2", "v1", "v2", "st"]
+
+_CACHE = {}
+
+
+def _rot(lst, i):
+    if not lst:
+        return []
+    i = i % len(lst)
+    return lst[i:] + lst[:i]
+
+
+def _split(lst, n):
+    out, k = [], 0
+    for j in range(n):
+        m = (len(lst) - k + (n - j - 1)) // (n - j)
+        out.append(lst[k:k + m])
+        k += m
+    return out
+
+
+def _plan(T, topo):
+    cores = list(T.cores)
+    hosts = max(topo.host(c) for c in cores) + 1
+    world = range(hosts * topo.CORES_PER_HOST)
+    by_chip = {}
+    for k in world:
+        by_chip.setdefault((topo.host(k), topo.chip(k)), []).append(k)
+    t_load, t_issue, t_lat, t_long, t_short = 2.0, 0.7, 1.5, 0.25, 0.7
+    sends, arrive = {}, {}
+
+    def pick(cands, die, dests, used):
+        for k in cands:
+            if k not in used and topo.die(k) == die and all(topo.may_write(k, d) for d in dests):
+                used.append(k)
+                return k
+        return None
+
+    for e, R in enumerate(cores):
+        rack = topo.rack(topo.host(R))
+        near = [d for d in cores if d != R and topo.rack(topo.host(d)) == rack]
+        far = [d for d in cores if topo.rack(topo.host(d)) != rack]
+        plane = [d for d in near if topo.same_plane(R, d)]
+        cross = [d for d in near if not topo.same_plane(R, d)]
+        place = sorted(plane + [R]).index(R)
+        other_die = [topo.die(k) for k in by_chip[(topo.host(R), topo.chip(R))] if topo.die(k) != topo.die(R)][0]
+        used = [R]
+        relays = []
+        fchip = [k for k in world if topo.rack(topo.host(k)) != rack and topo.chip(k) == topo.chip(R)
+                 and topo.may_write(R, k)]
+        fplane = _rot([d for d in far if topo.same_plane(fchip[0], d)], place)
+        fcross = _rot([d for d in far if not topo.same_plane(fchip[0], d)], place)
+        for part in _split(fcross, NFAR // 2):
+            relays.append((pick(fchip, other_die, part, used), part))
+        for part in _split(fplane, NFAR // 2):
+            relays.append((pick(fchip, topo.die(R), part, used), part))
+        for part in _split(_rot(cross, place), 2):
+            relays.append((pick(by_chip[(topo.host(R), topo.chip(R))], other_die, part, used), part))
+        grp = sorted(plane + [R])
+        mine = [grp[(place + 1 + s) % len(grp)] for s in range(len(plane))]
+        sends[R] = (e, [(k, True) for k, _ in relays] + [(d, False) for d in mine])
+        t = t_load + t_issue
+        got = {}
+        for d, is_relay in sends[R][1]:
+            t += t_long if is_relay else t_short
+            if is_relay:
+                got[d] = t + t_lat
+            else:
+                arrive[(e, d)] = t + t_lat
+        for k, part in relays:
+            sends[k] = (e, [(d, False) for d in part])
+            t = got[k] + t_issue
+            for d in part:
+                t += t_short
+                arrive[(e, d)] = t + t_lat
+        arrive[(e, R)] = 0.0
+    order = [sorted(range(len(cores)), key=lambda e: (arrive[(e, d)], e)) for d in cores]
+    return sends, order
+
+
+def _send(g, core, T, topo, e, dests):
+    mask = topo.mask(core, dests[0][0])
+    ids, aps = [], []
+    for d, is_relay in dests:
+        mask &= topo.mask(core, d)
+        rid, pid = topo.addr(d, core)
+        ids.append(DstId(rid=rid, pnc=pid))
+        aps.append(T.wd[:, :] if is_relay else T.wall[:, e * D:(e + 1) * D])
+    g.remote_dma_fused(
+        [RemoteDMATransfer(dst_ids=ids, dma_engine_mask=mask, remote_sem=T.sem["wa%d" % e], srcs=[T.wd[:, :]], dsts=aps)],
+        local_sem=T.sem.sent)
+    return bin(mask).count("1")
+
+
+def rank_program(g, core, T, topo):
+    if "plan" not in _CACHE:
+        _CACHE["plan"] = _plan(T, topo)
+    sends, order = _CACHE["plan"]
+    rank = T.rank_of(core)
+    if rank is None:
+        if core in sends:
+            e, dests = sends[core]
+            src = T.cores[e]
+            g.wait_ge(T.sem["wa%d" % e], bin(_mask_of(topo, src, sends[src][1])).count("1"))
+            n = _send(g, core, T, topo, e, dests)
+            g.wait_ge(T.sem.sent, n)
+        return
+
+    tok = T.tables["TOK"]
+    route = T.tables["ROUTE"][rank]
+    own = T.wall[:, rank * D:(rank + 1) * D]
+    g.sync.dma_start(T.wd[:, :], T.w[:, :]).then_inc(T.sem.wdl, 16)
+    g.scalar.dma_start(T.xs[:, :], T.x[:, :]).then_inc(T.sem.xl, 16)
+    g.scalar.dma_start(own, T.w[:, :]).then_inc(T.sem.wl, 16)
+    g.wait_ge(T.sem.wdl, 16)
+    nsent = _send(g, core, T, topo, rank, sends[core][1])
+
+    seq = order[rank]
+    pos = {e: i for i, e in enumerate(seq)}
+    jobs = {e: ([], []) for e in seq}
+    for t in range(tok):
+        a, b = route[t]
+        if pos[a] > pos[b]:
+            a, b = b, a
+        jobs[a][0].append(t)
+        jobs[b][1].append(t)
+    count = [0, 0]
+    banks = (T.p1, T.p2)
+    sems = (T.sem.m1, T.sem.m2)
+    g.tensor.wait_ge(T.sem.xl, 16)
+    for e in seq:
+        if not (jobs[e][0] or jobs[e][1]):
+            continue
+        if e == rank:
+            g.tensor.wait_ge(T.sem.wl, 16)
+        else:
+            g.tensor.wait_ge(T.sem["wa%d" % e], _arrival(topo, T, sends, e, core))
+        for b in (0, 1):
+            ts = jobs[e][b]
+            i = 0
+            while i < len(ts):
+                j = i
+                while j + 1 < len(ts) and ts[j + 1] == ts[j] + 1:
+                    j += 1
+                lo, hi = ts[i], ts[j] + 1
+                g.tensor.matmul(banks[b][:, lo:hi], T.wall[:, e * D:(e + 1) * D], T.xs[:, lo:hi],
+                                start=True, stop=True).then_inc(sems[b], 1)
+                count[b] += 1
+                i = j + 1
+
+    g.vector.wait_ge(T.sem.m1, count[0])
+    g.vector.tensor_copy(T.tmp[:, :], T.p1[:, 0:tok]).then_inc(T.sem.v1, 1)
+    g.vector.wait_ge(T.sem.m2, count[1])
+    g.vector.wait_ge(T.sem.v1, 1)
+    g.vector.tensor_tensor(T.ys[:, :], T.tmp[:, :], T.p2[:, 0:tok], AluOpType.add).then_inc(T.sem.v2, 1)
+    g.sync.wait_ge(T.sem.v2, 1)
+    g.sync.dma_start(T.y[:, :], T.ys[:, :]).then_inc(T.sem.st, 16)
+    g.sync.wait_ge(T.sem.st, 16)
+    g.wait_ge(T.sem.sent, nsent)
+
+
+def _mask_of(topo, src, dests):
+    mask = topo.mask(src, dests[0][0])
+    for d, _ in dests:
+        mask &= topo.mask(src, d)
+    return mask
+
+
+def _arrival(topo, T, sends, e, core):
+    for s, (ee, dests) in sends.items():
+        if ee == e and any(d == core for d, _ in dests):
+            return bin(_mask_of(topo, s, dests)).count("1")
+    return None

@@ -3,7 +3,8 @@ from concourse.mybir import AluOpType
 
 NEXP = 16
 D = 128
-NFAR = 2
+NFAR = 4
+NCROSS = 2
 SCRATCH = {
     "wall": ("sbuf", [D, NEXP * D], "bfloat16"),
     "wd": ("dram", [D, D], "bfloat16"),
@@ -41,7 +42,7 @@ def _plan(T, topo):
     by_chip = {}
     for k in world:
         by_chip.setdefault((topo.host(k), topo.chip(k)), []).append(k)
-    t_load, t_issue, t_lat, t_long, t_short = 2.0, 0.7, 1.5, 0.25, 0.7
+    t_load, t_issue, t_lat, t_long, t_short, t_cable = 2.0, 0.4, 0.4, 0.1, 0.3, 1.9
     sends, arrive = {}, {}
 
     def pick(cands, die, dests, used):
@@ -51,60 +52,88 @@ def _plan(T, topo):
                 return k
         return None
 
+    def clock(e, k, t_ready):
+        for tr in sends[k][1]:
+            t = t_ready + t_issue
+            for d, is_relay in tr:
+                if topo.rack(topo.host(d)) != topo.rack(topo.host(k)):
+                    t += t_cable
+                else:
+                    t += t_long if is_relay else t_short * len(sends[k][1])
+                if is_relay:
+                    clock(e, d, t + t_lat)
+                else:
+                    arrive[(e, d)] = t + t_lat
+
     for e, R in enumerate(cores):
         rack = topo.rack(topo.host(R))
         near = [d for d in cores if d != R and topo.rack(topo.host(d)) == rack]
         far = [d for d in cores if topo.rack(topo.host(d)) != rack]
         plane = [d for d in near if topo.same_plane(R, d)]
         cross = [d for d in near if not topo.same_plane(R, d)]
-        place = sorted(plane + [R]).index(R)
-        other_die = [topo.die(k) for k in by_chip[(topo.host(R), topo.chip(R))] if topo.die(k) != topo.die(R)][0]
+        grp = sorted(plane + [R])
+        place = grp.index(R)
+        home = by_chip[(topo.host(R), topo.chip(R))]
+        other_die = [topo.die(k) for k in home if topo.die(k) != topo.die(R)][0]
         used = [R]
-        relays = []
         fchip = [k for k in world if topo.rack(topo.host(k)) != rack and topo.chip(k) == topo.chip(R)
                  and topo.may_write(R, k)]
-        fplane = _rot([d for d in far if topo.same_plane(fchip[0], d)], place)
-        fcross = _rot([d for d in far if not topo.same_plane(fchip[0], d)], place)
-        for part in _split(fcross, NFAR // 2):
-            relays.append((pick(fchip, other_die, part, used), part))
-        for part in _split(fplane, NFAR // 2):
-            relays.append((pick(fchip, topo.die(R), part, used), part))
-        for part in _split(_rot(cross, place), 2):
-            relays.append((pick(by_chip[(topo.host(R), topo.chip(R))], other_die, part, used), part))
-        grp = sorted(plane + [R])
+        fplane = _split(_rot([d for d in far if topo.same_plane(fchip[0], d)], place), NFAR // 2)
+        fcross = _split(_rot([d for d in far if not topo.same_plane(fchip[0], d)], place), NFAR // 2)
+        head = pick(fchip, topo.die(R), fplane[0], used)
+        kids = []
+        for part in fcross:
+            kids.append((pick(fchip, other_die, part, used), part))
+        for part in fplane[1:]:
+            kids.append((pick(fchip, topo.die(R), part, used), part))
+        for k, part in kids:
+            sends[k] = (e, [[(d, False) for d in part]])
+        sends[head] = (e, [[(k, True) for k, _ in kids] + [(d, False) for d in fplane[0]]])
+        locs = []
+        for part in _split(_rot(cross, place), NCROSS):
+            locs.append((pick(home, other_die, part, used), part))
+        for k, part in locs:
+            sends[k] = (e, [[(d, False) for d in part]])
         mine = [grp[(place + 1 + s) % len(grp)] for s in range(len(plane))]
-        sends[R] = (e, [(k, True) for k, _ in relays] + [(d, False) for d in mine])
-        t = t_load + t_issue
-        got = {}
-        for d, is_relay in sends[R][1]:
-            t += t_long if is_relay else t_short
-            if is_relay:
-                got[d] = t + t_lat
-            else:
-                arrive[(e, d)] = t + t_lat
-        for k, part in relays:
-            sends[k] = (e, [(d, False) for d in part])
-            t = got[k] + t_issue
-            for d in part:
-                t += t_short
-                arrive[(e, d)] = t + t_lat
+        sends[R] = (e, [[(head, True)], [(k, True) for k, _ in locs] + [(d, False) for d in mine]])
+        clock(e, R, t_load)
         arrive[(e, R)] = 0.0
     order = [sorted(range(len(cores)), key=lambda e: (arrive[(e, d)], e)) for d in cores]
     return sends, order
 
 
-def _send(g, core, T, topo, e, dests):
-    mask = topo.mask(core, dests[0][0])
-    ids, aps = [], []
-    for d, is_relay in dests:
-        mask &= topo.mask(core, d)
-        rid, pid = topo.addr(d, core)
-        ids.append(DstId(rid=rid, pnc=pid))
-        aps.append(T.wd[:, :] if is_relay else T.wall[:, e * D:(e + 1) * D])
-    g.remote_dma_fused(
-        [RemoteDMATransfer(dst_ids=ids, dma_engine_mask=mask, remote_sem=T.sem["wa%d" % e], srcs=[T.wd[:, :]], dsts=aps)],
-        local_sem=T.sem.sent)
-    return bin(mask).count("1")
+def _masks(topo, src, transfers):
+    mask = topo.mask(src, transfers[0][0][0])
+    for tr in transfers:
+        for d, _ in tr:
+            mask &= topo.mask(src, d)
+    bits = [1 << i for i in range(mask.bit_length()) if mask >> i & 1]
+    share = len(bits) // len(transfers)
+    return [sum(bits[j * share:(j + 1) * share]) for j in range(len(transfers))]
+
+
+def _send(g, core, T, topo, e, transfers):
+    masks = _masks(topo, core, transfers)
+    lst = []
+    for tr, mask in zip(transfers, masks):
+        ids, aps = [], []
+        for d, is_relay in tr:
+            rid, pid = topo.addr(d, core)
+            ids.append(DstId(rid=rid, pnc=pid))
+            aps.append(T.wd[:, :] if is_relay else T.wall[:, e * D:(e + 1) * D])
+        lst.append(RemoteDMATransfer(dst_ids=ids, dma_engine_mask=mask, remote_sem=T.sem["wa%d" % e],
+                                     srcs=[T.wd[:, :]], dsts=aps))
+    g.remote_dma_fused(lst, local_sem=T.sem.sent)
+    return sum(bin(m).count("1") for m in masks)
+
+
+def _arrival(topo, sends, e, core):
+    for s, (ee, transfers) in sends.items():
+        if ee == e:
+            for tr, mask in zip(transfers, _masks(topo, s, transfers)):
+                if any(d == core for d, _ in tr):
+                    return bin(mask).count("1")
+    return None
 
 
 def rank_program(g, core, T, topo):
@@ -115,8 +144,7 @@ def rank_program(g, core, T, topo):
     if rank is None:
         if core in sends:
             e, dests = sends[core]
-            src = T.cores[e]
-            g.wait_ge(T.sem["wa%d" % e], bin(_mask_of(topo, src, sends[src][1])).count("1"))
+            g.wait_ge(T.sem["wa%d" % e], _arrival(topo, sends, e, core))
             n = _send(g, core, T, topo, e, dests)
             g.wait_ge(T.sem.sent, n)
         return
@@ -144,12 +172,10 @@ def rank_program(g, core, T, topo):
     sems = (T.sem.m1, T.sem.m2)
     g.tensor.wait_ge(T.sem.xl, 16)
     for e in seq:
-        if not (jobs[e][0] or jobs[e][1]):
-            continue
         if e == rank:
             g.tensor.wait_ge(T.sem.wl, 16)
         else:
-            g.tensor.wait_ge(T.sem["wa%d" % e], _arrival(topo, T, sends, e, core))
+            g.tensor.wait_ge(T.sem["wa%d" % e], _arrival(topo, sends, e, core))
         for b in (0, 1):
             ts = jobs[e][b]
             i = 0
@@ -172,17 +198,3 @@ def rank_program(g, core, T, topo):
     g.sync.dma_start(T.y[:, :], T.ys[:, :]).then_inc(T.sem.st, 16)
     g.sync.wait_ge(T.sem.st, 16)
     g.wait_ge(T.sem.sent, nsent)
-
-
-def _mask_of(topo, src, dests):
-    mask = topo.mask(src, dests[0][0])
-    for d, _ in dests:
-        mask &= topo.mask(src, d)
-    return mask
-
-
-def _arrival(topo, T, sends, e, core):
-    for s, (ee, dests) in sends.items():
-        if ee == e and any(d == core for d, _ in dests):
-            return bin(_mask_of(topo, s, dests)).count("1")
-    return None

@@ -9,12 +9,13 @@ SCRATCH = {
     "wall": ("sbuf", [D, NEXP * D], "bfloat16"),
     "wd": ("dram", [D, D], "bfloat16"),
     "xs": ("sbuf", [D, 64], "bfloat16"),
-    "tmp": ("sbuf", [D, 64], "float32"),
+    "xm": ("sbuf", [D, NEXP * 64], "bfloat16"),
+    "zz": ("sbuf", [D, D], "bfloat16"),
     "ys": ("sbuf", [D, 64], "bfloat16"),
-    "p1": ("psum", [D, 512], "float32"),
-    "p2": ("psum", [D, 512], "float32"),
+    "ps": ("psum", [D, 512], "float32"),
 }
-SEMAPHORES = ["wa%d" % e for e in range(NEXP)] + ["wdl", "wl", "xl", "sent", "m1", "m2", "v1", "v2", "st"]
+SEMAPHORES = (["wa%d" % e for e in range(NEXP)] + ["xk%d" % e for e in range(NEXP)]
+              + ["wdl", "wl", "xl", "sent", "zs", "mm", "v2", "st"])
 
 _CACHE = {}
 
@@ -32,6 +33,17 @@ def _split(lst, n):
         m = (len(lst) - k + (n - j - 1)) // (n - j)
         out.append(lst[k:k + m])
         k += m
+    return out
+
+
+def _runs(ts):
+    out, i = [], 0
+    while i < len(ts):
+        j = i
+        while j + 1 < len(ts) and ts[j + 1] == ts[j] + 1:
+            j += 1
+        out.append((ts[i], ts[j] + 1))
+        i = j + 1
     return out
 
 
@@ -159,41 +171,40 @@ def rank_program(g, core, T, topo):
     nsent = _send(g, core, T, topo, rank, sends[core][1])
 
     seq = order[rank]
-    pos = {e: i for i, e in enumerate(seq)}
-    jobs = {e: ([], []) for e in seq}
-    for t in range(tok):
-        a, b = route[t]
-        if pos[a] > pos[b]:
-            a, b = b, a
-        jobs[a][0].append(t)
-        jobs[b][1].append(t)
-    count = [0, 0]
-    banks = (T.p1, T.p2)
-    sems = (T.sem.m1, T.sem.m2)
-    g.tensor.wait_ge(T.sem.xl, 16)
-    for e in seq:
-        if e == rank:
-            g.tensor.wait_ge(T.sem.wl, 16)
-        else:
-            g.tensor.wait_ge(T.sem["wa%d" % e], _arrival(topo, sends, e, core))
-        for b in (0, 1):
-            ts = jobs[e][b]
-            i = 0
-            while i < len(ts):
-                j = i
-                while j + 1 < len(ts) and ts[j + 1] == ts[j] + 1:
-                    j += 1
-                lo, hi = ts[i], ts[j] + 1
-                g.tensor.matmul(banks[b][:, lo:hi], T.wall[:, e * D:(e + 1) * D], T.xs[:, lo:hi],
-                                start=True, stop=True).then_inc(sems[b], 1)
-                count[b] += 1
-                i = j + 1
+    my_rack = topo.rack(topo.host(core))
+    late = [e for e in seq if topo.rack(topo.host(T.cores[e])) != my_rack]
+    runs = {e: _runs([t for t in range(tok) for r in route[t] if r == e]) for e in seq}
 
-    g.vector.wait_ge(T.sem.m1, count[0])
-    g.vector.tensor_copy(T.tmp[:, :], T.p1[:, 0:tok]).then_inc(T.sem.v1, 1)
-    g.vector.wait_ge(T.sem.m2, count[1])
-    g.vector.wait_ge(T.sem.v1, 1)
-    g.vector.tensor_tensor(T.ys[:, :], T.tmp[:, :], T.p2[:, 0:tok], AluOpType.add).then_inc(T.sem.v2, 1)
+    lo_slot, hi_slot = min(late) * tok, (max(late) + 1) * tok
+    g.vector.memset(T.zz[:, :], 0.0).then_inc(T.sem.zs, 1)
+    g.vector.memset(T.xm[:, lo_slot:hi_slot], 0.0).then_inc(T.sem.zs, 1)
+    g.vector.wait_ge(T.sem.zs, 2)
+    g.vector.wait_ge(T.sem.xl, 16)
+    for e in late:
+        for lo, hi in runs[e]:
+            g.vector.tensor_copy(T.xm[:, e * tok + lo:e * tok + hi], T.xs[:, lo:hi]).then_inc(T.sem["xk%d" % e], 1)
+
+    todo = []
+    for e in seq:
+        w_e = T.wall[:, e * D:(e + 1) * D]
+        waits = [(T.sem.wl, 16)] if e == rank else [(T.sem["wa%d" % e], _arrival(topo, sends, e, core))]
+        if e in late:
+            waits.append((T.sem["xk%d" % e], len(runs[e])))
+            todo.append((waits, w_e, T.xm[:, e * tok:(e + 1) * tok], T.ps[:, 0:tok]))
+        else:
+            for lo, hi in runs[e]:
+                todo.append((waits, w_e, T.xs[:, lo:hi], T.ps[:, lo:hi]))
+                waits = []
+    g.tensor.wait_ge(T.sem.zs, 2)
+    g.tensor.matmul(T.ps[:, 0:tok], T.zz[:, :], T.zz[:, 0:tok], start=True, stop=False).then_inc(T.sem.mm, 1)
+    g.tensor.wait_ge(T.sem.xl, 16)
+    for i, (waits, lhsT, rhs, out) in enumerate(todo):
+        for sem, val in waits:
+            g.tensor.wait_ge(sem, val)
+        g.tensor.matmul(out, lhsT, rhs, start=False, stop=(i == len(todo) - 1)).then_inc(T.sem.mm, 1)
+
+    g.vector.wait_ge(T.sem.mm, len(todo) + 1)
+    g.vector.tensor_copy(T.ys[:, :], T.ps[:, 0:tok]).then_inc(T.sem.v2, 1)
     g.sync.wait_ge(T.sem.v2, 1)
     g.sync.dma_start(T.y[:, :], T.ys[:, :]).then_inc(T.sem.st, 16)
     g.sync.wait_ge(T.sem.st, 16)

@@ -1,21 +1,24 @@
 from concourse.bass import DstId, RemoteDMATransfer
-from concourse.mybir import AluOpType
 
 NEXP = 16
 D = 128
+H = D // 2
 NFAR = 4
 NCROSS = 2
 SCRATCH = {
     "wall": ("sbuf", [D, NEXP * D], "bfloat16"),
     "wd": ("dram", [D, D], "bfloat16"),
+    "wda": ("dram", [D, H], "bfloat16"),
+    "wdb": ("dram", [D, H], "bfloat16"),
     "xs": ("sbuf", [D, 64], "bfloat16"),
     "xm": ("sbuf", [D, NEXP * 64], "bfloat16"),
     "zz": ("sbuf", [D, D], "bfloat16"),
     "ys": ("sbuf", [D, 64], "bfloat16"),
     "ps": ("psum", [D, 512], "float32"),
 }
-SEMAPHORES = (["wa%d" % e for e in range(NEXP)] + ["xk%d" % e for e in range(NEXP)]
-              + ["wdl", "wl", "xl", "sent", "zs", "mm", "v2", "st"])
+PIECES = {"F": "wa%d", "A": "wb%d", "B": "wc%d"}
+SEMAPHORES = ([p % e for p in PIECES.values() for e in range(NEXP)] + ["xk%d" % e for e in range(NEXP)]
+              + ["lf", "la", "lb", "wl", "xl", "sent", "zs", "mm", "v2", "st"])
 
 _CACHE = {}
 
@@ -47,6 +50,10 @@ def _runs(ts):
     return out
 
 
+def _bits(mask):
+    return [1 << i for i in range(mask.bit_length()) if mask >> i & 1]
+
+
 def _plan(T, topo):
     cores = list(T.cores)
     hosts = max(topo.host(c) for c in cores) + 1
@@ -54,7 +61,6 @@ def _plan(T, topo):
     by_chip = {}
     for k in world:
         by_chip.setdefault((topo.host(k), topo.chip(k)), []).append(k)
-    t_load, t_issue, t_lat, t_long, t_short, t_cable = 2.0, 0.4, 0.4, 0.1, 0.3, 1.9
     sends, arrive = {}, {}
 
     def pick(cands, die, dests, used):
@@ -63,19 +69,6 @@ def _plan(T, topo):
                 used.append(k)
                 return k
         return None
-
-    def clock(e, k, t_ready):
-        for tr in sends[k][1]:
-            t = t_ready + t_issue
-            for d, is_relay in tr:
-                if topo.rack(topo.host(d)) != topo.rack(topo.host(k)):
-                    t += t_cable
-                else:
-                    t += t_long if is_relay else t_short * len(sends[k][1])
-                if is_relay:
-                    clock(e, d, t + t_lat)
-                else:
-                    arrive[(e, d)] = t + t_lat
 
     for e, R in enumerate(cores):
         rack = topo.rack(topo.host(R))
@@ -98,53 +91,67 @@ def _plan(T, topo):
             kids.append((pick(fchip, other_die, part, used), part))
         for part in fplane[1:]:
             kids.append((pick(fchip, topo.die(R), part, used), part))
-        for k, part in kids:
-            sends[k] = (e, [[(d, False) for d in part]])
-        sends[head] = (e, [[(k, True) for k, _ in kids] + [(d, False) for d in fplane[0]]])
         locs = []
         for part in _split(_rot(cross, place), NCROSS):
             locs.append((pick(home, other_die, part, used), part))
-        for k, part in locs:
-            sends[k] = (e, [[(d, False) for d in part]])
         mine = [grp[(place + 1 + s) % len(grp)] for s in range(len(plane))]
-        sends[R] = (e, [[(head, True)], [(k, True) for k, _ in locs] + [(d, False) for d in mine]])
-        clock(e, R, t_load)
+        for k, part in kids:
+            call = [([(d, False) for d in part], topo.mask(k, part[0]))]
+            sends[k] = (e, [("A", [call]), ("B", [call])])
+        for k, part in locs:
+            sends[k] = (e, [("F", [[([(d, False) for d in part], topo.mask(k, part[0]))]])])
+        hcalls = [[([(k, True) for k, _ in kids], topo.mask(head, kids[0][0]))],
+                  [([(d, False) for d in fplane[0]], topo.mask(head, fplane[0][0]))]]
+        sends[head] = (e, [("A", hcalls), ("B", hcalls)])
+        out = _bits(topo.mask(R, head))
+        inner = topo.mask(R, locs[0][0]) & ~topo.mask(R, head)
+        cable = [[([(head, True)], sum(out[:len(out) // 2]))]]
+        sends[R] = (e, [("A", cable), ("B", cable),
+                        ("F", [[([(k, True) for k, _ in locs], inner),
+                                ([(d, False) for d in mine], sum(out[len(out) // 2:]))]])])
         arrive[(e, R)] = 0.0
+        for i, d in enumerate(mine):
+            arrive[(e, d)] = 10 + 0.3 * i
+        for k, part in locs:
+            for i, d in enumerate(part):
+                arrive[(e, d)] = 11 + 0.3 * i
+        for i, d in enumerate(fplane[0]):
+            arrive[(e, d)] = 100 + 0.3 * i
+        for k, part in kids:
+            for i, d in enumerate(part):
+                arrive[(e, d)] = 101 + 0.3 * i
     order = [sorted(range(len(cores)), key=lambda e: (arrive[(e, d)], e)) for d in cores]
     return sends, order
 
 
-def _masks(topo, src, transfers):
-    mask = topo.mask(src, transfers[0][0][0])
-    for tr in transfers:
-        for d, _ in tr:
-            mask &= topo.mask(src, d)
-    bits = [1 << i for i in range(mask.bit_length()) if mask >> i & 1]
-    share = len(bits) // len(transfers)
-    return [sum(bits[j * share:(j + 1) * share]) for j in range(len(transfers))]
+def _send(g, core, T, topo, e, piece, calls):
+    src = {"F": T.wd, "A": T.wda, "B": T.wdb}[piece]
+    lo, hi = {"F": (0, D), "A": (0, H), "B": (H, D)}[piece]
+    total = 0
+    for call in calls:
+        lst = []
+        for dests, mask in call:
+            ids, aps = [], []
+            for d, is_relay in dests:
+                rid, pid = topo.addr(d, core)
+                ids.append(DstId(rid=rid, pnc=pid))
+                aps.append(src[:, :] if is_relay else T.wall[:, e * D + lo:e * D + hi])
+            lst.append(RemoteDMATransfer(dst_ids=ids, dma_engine_mask=mask, remote_sem=T.sem[PIECES[piece] % e],
+                                         srcs=[src[:, :]], dsts=aps))
+            total += len(_bits(mask))
+        g.remote_dma_fused(lst, local_sem=T.sem.sent)
+    return total
 
 
-def _send(g, core, T, topo, e, transfers):
-    masks = _masks(topo, core, transfers)
-    lst = []
-    for tr, mask in zip(transfers, masks):
-        ids, aps = [], []
-        for d, is_relay in tr:
-            rid, pid = topo.addr(d, core)
-            ids.append(DstId(rid=rid, pnc=pid))
-            aps.append(T.wd[:, :] if is_relay else T.wall[:, e * D:(e + 1) * D])
-        lst.append(RemoteDMATransfer(dst_ids=ids, dma_engine_mask=mask, remote_sem=T.sem["wa%d" % e],
-                                     srcs=[T.wd[:, :]], dsts=aps))
-    g.remote_dma_fused(lst, local_sem=T.sem.sent)
-    return sum(bin(m).count("1") for m in masks)
-
-
-def _arrival(topo, sends, e, core):
-    for s, (ee, transfers) in sends.items():
+def _arrival(sends, e, piece, core):
+    for s, (ee, steps) in sends.items():
         if ee == e:
-            for tr, mask in zip(transfers, _masks(topo, s, transfers)):
-                if any(d == core for d, _ in tr):
-                    return bin(mask).count("1")
+            for p, calls in steps:
+                if p == piece:
+                    for call in calls:
+                        for dests, mask in call:
+                            if any(d == core for d, _ in dests):
+                                return len(_bits(mask))
     return None
 
 
@@ -155,20 +162,27 @@ def rank_program(g, core, T, topo):
     rank = T.rank_of(core)
     if rank is None:
         if core in sends:
-            e, dests = sends[core]
-            g.wait_ge(T.sem["wa%d" % e], _arrival(topo, sends, e, core))
-            n = _send(g, core, T, topo, e, dests)
+            e, steps = sends[core]
+            n = 0
+            for piece, calls in steps:
+                g.wait_ge(T.sem[PIECES[piece] % e], _arrival(sends, e, piece, core))
+                n += _send(g, core, T, topo, e, piece, calls)
             g.wait_ge(T.sem.sent, n)
         return
 
     tok = T.tables["TOK"]
     route = T.tables["ROUTE"][rank]
     own = T.wall[:, rank * D:(rank + 1) * D]
-    g.sync.dma_start(T.wd[:, :], T.w[:, :]).then_inc(T.sem.wdl, 16)
+    g.sync.dma_start(T.wda[:, :], T.w[:, 0:H]).then_inc(T.sem.la, 16)
+    g.sync.dma_start(T.wdb[:, :], T.w[:, H:D]).then_inc(T.sem.lb, 16)
+    g.sync.dma_start(T.wd[:, :], T.w[:, :]).then_inc(T.sem.lf, 16)
     g.scalar.dma_start(T.xs[:, :], T.x[:, :]).then_inc(T.sem.xl, 16)
     g.scalar.dma_start(own, T.w[:, :]).then_inc(T.sem.wl, 16)
-    g.wait_ge(T.sem.wdl, 16)
-    nsent = _send(g, core, T, topo, rank, sends[core][1])
+    loaded = {"A": T.sem.la, "B": T.sem.lb, "F": T.sem.lf}
+    nsent = 0
+    for piece, calls in sends[core][1]:
+        g.wait_ge(loaded[piece], 16)
+        nsent += _send(g, core, T, topo, rank, piece, calls)
 
     seq = order[rank]
     my_rack = topo.rack(topo.host(core))
@@ -186,22 +200,26 @@ def rank_program(g, core, T, topo):
 
     todo = []
     for e in seq:
-        w_e = T.wall[:, e * D:(e + 1) * D]
-        waits = [(T.sem.wl, 16)] if e == rank else [(T.sem["wa%d" % e], _arrival(topo, sends, e, core))]
         if e in late:
-            waits.append((T.sem["xk%d" % e], len(runs[e])))
-            todo.append((waits, w_e, T.xm[:, e * tok:(e + 1) * tok], T.ps[:, 0:tok]))
-        else:
-            for lo, hi in runs[e]:
-                todo.append((waits, w_e, T.xs[:, lo:hi], T.ps[:, lo:hi]))
-                waits = []
+            continue
+        waits = [(T.sem.wl, 16)] if e == rank else [(T.sem[PIECES["F"] % e], _arrival(sends, e, "F", core))]
+        for lo, hi in runs[e]:
+            todo.append((waits, T.wall[:, e * D:(e + 1) * D], T.xs[:, lo:hi], T.ps[:, lo:hi], False))
+            waits = []
+    for piece, lo, hi in (("A", 0, H), ("B", H, D)):
+        for e in late:
+            waits = [(T.sem[PIECES[piece] % e], _arrival(sends, e, piece, core))]
+            if piece == "A":
+                waits.append((T.sem["xk%d" % e], len(runs[e])))
+            todo.append((waits, T.wall[:, e * D + lo:e * D + hi], T.xm[:, e * tok:(e + 1) * tok], T.ps[lo:hi, 0:tok],
+                         e == late[-1]))
     g.tensor.wait_ge(T.sem.zs, 2)
     g.tensor.matmul(T.ps[:, 0:tok], T.zz[:, :], T.zz[:, 0:tok], start=True, stop=False).then_inc(T.sem.mm, 1)
     g.tensor.wait_ge(T.sem.xl, 16)
-    for i, (waits, lhsT, rhs, out) in enumerate(todo):
+    for waits, lhsT, rhs, out, stop in todo:
         for sem, val in waits:
             g.tensor.wait_ge(sem, val)
-        g.tensor.matmul(out, lhsT, rhs, start=False, stop=(i == len(todo) - 1)).then_inc(T.sem.mm, 1)
+        g.tensor.matmul(out, lhsT, rhs, start=False, stop=stop).then_inc(T.sem.mm, 1)
 
     g.vector.wait_ge(T.sem.mm, len(todo) + 1)
     g.vector.tensor_copy(T.ys[:, :], T.ps[:, 0:tok]).then_inc(T.sem.v2, 1)

from concourse.bass import DstId, RemoteDMATransfer

NEXP = 16
D = 128
H = D // 2
NFAR = 4
NCROSS = 2
SCRATCH = {
    "wall": ("sbuf", [D, NEXP * D], "bfloat16"),
    "wd": ("dram", [D, D], "bfloat16"),
    "wda": ("dram", [D, H], "bfloat16"),
    "wdb": ("dram", [D, H], "bfloat16"),
    "xs": ("sbuf", [D, 64], "bfloat16"),
    "xm": ("sbuf", [D, NEXP * 64], "bfloat16"),
    "zz": ("sbuf", [D, D], "bfloat16"),
    "ys": ("sbuf", [D, 64], "bfloat16"),
    "ps": ("psum", [D, 512], "float32"),
}
PIECES = {"F": "wa%d", "A": "wb%d", "B": "wc%d"}
SEMAPHORES = ([p % e for p in PIECES.values() for e in range(NEXP)] + ["xk%d" % e for e in range(NEXP)]
              + ["lf", "la", "lb", "wl", "xl", "sent", "zs", "mm", "v2", "st"])

_CACHE = {}


def _rot(lst, i):
    if not lst:
        return []
    i = i % len(lst)
    return lst[i:] + lst[:i]


def _split(lst, n):
    out, k = [], 0
    for j in range(n):
        m = (len(lst) - k + (n - j - 1)) // (n - j)
        out.append(lst[k:k + m])
        k += m
    return out


def _runs(ts):
    out, i = [], 0
    while i < len(ts):
        j = i
        while j + 1 < len(ts) and ts[j + 1] == ts[j] + 1:
            j += 1
        out.append((ts[i], ts[j] + 1))
        i = j + 1
    return out


def _bits(mask):
    return [1 << i for i in range(mask.bit_length()) if mask >> i & 1]


def _plan(T, topo):
    cores = list(T.cores)
    hosts = max(topo.host(c) for c in cores) + 1
    world = range(hosts * topo.CORES_PER_HOST)
    by_chip = {}
    for k in world:
        by_chip.setdefault((topo.host(k), topo.chip(k)), []).append(k)
    sends, arrive = {}, {}

    def pick(cands, die, dests, used):
        for k in cands:
            if k not in used and topo.die(k) == die and all(topo.may_write(k, d) for d in dests):
                used.append(k)
                return k
        return None

    for e, R in enumerate(cores):
        rack = topo.rack(topo.host(R))
        near = [d for d in cores if d != R and topo.rack(topo.host(d)) == rack]
        far = [d for d in cores if topo.rack(topo.host(d)) != rack]
        plane = [d for d in near if topo.same_plane(R, d)]
        cross = [d for d in near if not topo.same_plane(R, d)]
        grp = sorted(plane + [R])
        place = grp.index(R)
        home = by_chip[(topo.host(R), topo.chip(R))]
        other_die = [topo.die(k) for k in home if topo.die(k) != topo.die(R)][0]
        used = [R]
        fchip = [k for k in world if topo.rack(topo.host(k)) != rack and topo.chip(k) == topo.chip(R)
                 and topo.may_write(R, k)]
        fplane = _split(_rot([d for d in far if topo.same_plane(fchip[0], d)], place), NFAR // 2)
        fcross = _split(_rot([d for d in far if not topo.same_plane(fchip[0], d)], place), NFAR // 2)
        head = pick(fchip, topo.die(R), fplane[0], used)
        kids = []
        for part in fcross:
            kids.append((pick(fchip, other_die, part, used), part))
        for part in fplane[1:]:
            kids.append((pick(fchip, topo.die(R), part, used), part))
        locs = []
        for part in _split(_rot(cross, place), NCROSS):
            locs.append((pick(home, other_die, part, used), part))
        mine = [grp[(place + 1 + s) % len(grp)] for s in range(len(plane))]
        for k, part in kids:
            call = [([(d, False) for d in part], topo.mask(k, part[0]))]
            sends[k] = (e, [("A", [call]), ("B", [call])])
        for k, part in locs:
            sends[k] = (e, [("F", [[([(d, False) for d in part], topo.mask(k, part[0]))]])])
        hcalls = [[([(k, True) for k, _ in kids], topo.mask(head, kids[0][0]))],
                  [([(d, False) for d in fplane[0]], topo.mask(head, fplane[0][0]))]]
        sends[head] = (e, [("A", hcalls), ("B", hcalls)])
        out = _bits(topo.mask(R, head))
        inner = topo.mask(R, locs[0][0]) & ~topo.mask(R, head)
        cable = [[([(head, True)], sum(out[:len(out) // 2]))]]
        sends[R] = (e, [("A", cable), ("B", cable),
                        ("F", [[([(k, True) for k, _ in locs], inner),
                                ([(d, False) for d in mine], sum(out[len(out) // 2:]))]])])
        arrive[(e, R)] = 0.0
        for i, d in enumerate(mine):
            arrive[(e, d)] = 10 + 0.3 * i
        for k, part in locs:
            for i, d in enumerate(part):
                arrive[(e, d)] = 11 + 0.3 * i
        for i, d in enumerate(fplane[0]):
            arrive[(e, d)] = 100 + 0.3 * i
        for k, part in kids:
            for i, d in enumerate(part):
                arrive[(e, d)] = 101 + 0.3 * i
    order = [sorted(range(len(cores)), key=lambda e: (arrive[(e, d)], e)) for d in cores]
    return sends, order


def _send(g, core, T, topo, e, piece, calls):
    src = {"F": T.wd, "A": T.wda, "B": T.wdb}[piece]
    lo, hi = {"F": (0, D), "A": (0, H), "B": (H, D)}[piece]
    total = 0
    for call in calls:
        lst = []
        for dests, mask in call:
            ids, aps = [], []
            for d, is_relay in dests:
                rid, pid = topo.addr(d, core)
                ids.append(DstId(rid=rid, pnc=pid))
                aps.append(src[:, :] if is_relay else T.wall[:, e * D + lo:e * D + hi])
            lst.append(RemoteDMATransfer(dst_ids=ids, dma_engine_mask=mask, remote_sem=T.sem[PIECES[piece] % e],
                                         srcs=[src[:, :]], dsts=aps))
            total += len(_bits(mask))
        g.remote_dma_fused(lst, local_sem=T.sem.sent)
    return total


def _arrival(sends, e, piece, core):
    for s, (ee, steps) in sends.items():
        if ee == e:
            for p, calls in steps:
                if p == piece:
                    for call in calls:
                        for dests, mask in call:
                            if any(d == core for d, _ in dests):
                                return len(_bits(mask))
    return None


def rank_program(g, core, T, topo):
    if "plan" not in _CACHE:
        _CACHE["plan"] = _plan(T, topo)
    sends, order = _CACHE["plan"]
    rank = T.rank_of(core)
    if rank is None:
        if core in sends:
            e, steps = sends[core]
            n = 0
            for piece, calls in steps:
                g.wait_ge(T.sem[PIECES[piece] % e], _arrival(sends, e, piece, core))
                n += _send(g, core, T, topo, e, piece, calls)
            g.wait_ge(T.sem.sent, n)
        return

    tok = T.tables["TOK"]
    route = T.tables["ROUTE"][rank]
    own = T.wall[:, rank * D:(rank + 1) * D]
    g.sync.dma_start(T.wda[:, :], T.w[:, 0:H]).then_inc(T.sem.la, 16)
    g.sync.dma_start(T.wdb[:, :], T.w[:, H:D]).then_inc(T.sem.lb, 16)
    g.sync.dma_start(T.wd[:, :], T.w[:, :]).then_inc(T.sem.lf, 16)
    g.scalar.dma_start(T.xs[:, :], T.x[:, :]).then_inc(T.sem.xl, 16)
    g.scalar.dma_start(own, T.w[:, :]).then_inc(T.sem.wl, 16)
    loaded = {"A": T.sem.la, "B": T.sem.lb, "F": T.sem.lf}
    nsent = 0
    for piece, calls in sends[core][1]:
        g.wait_ge(loaded[piece], 16)
        nsent += _send(g, core, T, topo, rank, piece, calls)

    seq = order[rank]
    my_rack = topo.rack(topo.host(core))
    late = [e for e in seq if topo.rack(topo.host(T.cores[e])) != my_rack]
    runs = {e: _runs([t for t in range(tok) for r in route[t] if r == e]) for e in seq}

    lo_slot, hi_slot = min(late) * tok, (max(late) + 1) * tok
    g.vector.memset(T.zz[:, :], 0.0).then_inc(T.sem.zs, 1)
    g.vector.memset(T.xm[:, lo_slot:hi_slot], 0.0).then_inc(T.sem.zs, 1)
    g.vector.wait_ge(T.sem.zs, 2)
    g.vector.wait_ge(T.sem.xl, 16)
    for e in late:
        for lo, hi in runs[e]:
            g.vector.tensor_copy(T.xm[:, e * tok + lo:e * tok + hi], T.xs[:, lo:hi]).then_inc(T.sem["xk%d" % e], 1)

    todo = []
    for e in seq:
        if e in late:
            continue
        waits = [(T.sem.wl, 16)] if e == rank else [(T.sem[PIECES["F"] % e], _arrival(sends, e, "F", core))]
        for lo, hi in runs[e]:
            todo.append((waits, T.wall[:, e * D:(e + 1) * D], T.xs[:, lo:hi], T.ps[:, lo:hi], False))
            waits = []
    for piece, lo, hi in (("A", 0, H), ("B", H, D)):
        for e in late:
            waits = [(T.sem[PIECES[piece] % e], _arrival(sends, e, piece, core))]
            if piece == "A":
                waits.append((T.sem["xk%d" % e], len(runs[e])))
            todo.append((waits, T.wall[:, e * D + lo:e * D + hi], T.xm[:, e * tok:(e + 1) * tok], T.ps[lo:hi, 0:tok],
                         e == late[-1]))
    g.tensor.wait_ge(T.sem.zs, 2)
    g.tensor.matmul(T.ps[:, 0:tok], T.zz[:, :], T.zz[:, 0:tok], start=True, stop=False).then_inc(T.sem.mm, 1)
    g.tensor.wait_ge(T.sem.xl, 16)
    for waits, lhsT, rhs, out, stop in todo:
        for sem, val in waits:
            g.tensor.wait_ge(sem, val)
        g.tensor.matmul(out, lhsT, rhs, start=False, stop=stop).then_inc(T.sem.mm, 1)

    g.vector.wait_ge(T.sem.mm, len(todo) + 1)
    g.vector.tensor_copy(T.ys[:, :], T.ps[:, 0:tok]).then_inc(T.sem.v2, 1)
    g.sync.wait_ge(T.sem.v2, 1)
    g.sync.dma_start(T.y[:, :], T.ys[:, :]).then_inc(T.sem.st, 16)
    g.sync.wait_ge(T.sem.st, 16)
    g.wait_ge(T.sem.sent, nsent)
